import numpy as np
import ml_dtypes


def mxq(x, axis, fmt="e4m3"):
    dtype, down = {"e4m3": (ml_dtypes.float8_e4m3fn, 7), "e5m2": (ml_dtypes.float8_e5m2, 14)}[fmt]
    v = np.moveaxis(np.asarray(x, np.float32).astype(ml_dtypes.bfloat16).astype(np.float64), axis, -1)
    blocks = v.reshape(v.shape[:-1] + (-1, 32))
    amax = np.abs(blocks).max(-1, keepdims=True)
    byte = np.maximum(np.where(amax > 0, np.frexp(amax)[1] - 1 + 127, 0) - down, 1)
    scale = np.exp2(byte - 127.0)
    codes = (blocks / scale).astype(np.float32).astype(dtype).astype(np.float64)
    return np.moveaxis((codes * scale).reshape(v.shape), -1, axis)


WIDE = False


def mx_kscale(k):
    if not WIDE:
        return np.ones(k)
    levels = np.array([10, -10, 5, -5, 0])
    if k % 512:
        return np.exp2(np.random.permutation(np.resize(levels, k // 32))).repeat(32)
    a = np.empty((k // 512, 16))
    for p in range(k // 512):
        a[p, :8] = np.random.permutation(np.resize(levels, 8))
        for g in range(8):
            far = levels[np.abs(levels - a[p, g]) >= 10]
            a[p, g + 8] = far[np.random.randint(len(far))]
    return np.exp2(a.ravel()).repeat(32)


BF16 = ml_dtypes.bfloat16


def bf(x):
    return np.asarray(x, np.float32).astype(BF16)


def f64(x):
    return np.asarray(x).astype(np.float64)

def planes(Y):
    n, m = Y.shape
    b = f64(bf(Y)).reshape(n // 32, 32, m)
    amax = np.abs(b).max(1)
    byte = np.clip(np.where(amax > 0, np.frexp(amax)[1] - 1 + 127 - 7, 1), 1, 254)
    codes = (b * np.exp2(127.0 - byte)[:, None, :]).reshape(n, m).astype(np.float32).astype(ml_dtypes.float8_e4m3fn).view(np.uint8)
    words = codes.reshape(n // 512, 128, 4, m).transpose(0, 1, 3, 2)
    return np.ascontiguousarray(words), np.ascontiguousarray(byte.astype(np.uint8).reshape(n // 512, 16, m))


E, C, D, F = 4, 512, 1024, 1536


def setup_inputs():
    s = mx_kscale(D)
    x = np.random.randn(E, C, D) * s
    w_up = np.random.randn(E, D, F) / np.sqrt(D) / s[:, None]
    base = np.exp(0.7 * np.random.randn(E, F))
    limit = 1.25 * base * np.exp(0.1 * np.random.randn(E, F))
    return {
        "x": bf(x),
        "w_up": bf(w_up),
        "ch_scale": bf(base),
        "ch_limit": bf(limit),
    }


def reference(x, w_up, ch_scale, ch_limit):
    xq = mxq(f64(x), 2, "e4m3")
    wq = mxq(f64(w_up), 1, "e4m3")
    z = wq.swapaxes(1, 2) @ xq.swapaxes(1, 2)
    h = z * f64(ch_scale)[:, :, None]
    a = h / (1.0 + np.exp(-h))
    y = np.minimum(a, f64(ch_limit)[:, :, None])
    Y = y.transpose(1, 0, 2).reshape(F, E * C)
    words, scales = planes(Y)
    return y, words, scales

@@ -1,0 +1,237 @@
+from contextlib import ExitStack
+
+import concourse.mybir as mybir
+from concourse.masks import make_identity
+
+E, C, D, F = 4, 512, 1024, 1536
+FLOPS = 2 * E * C * D * F
+
+F32 = mybir.dt.float32
+BF16 = mybir.dt.bfloat16
+U32 = mybir.dt.uint32
+I32 = mybir.dt.int32
+U8 = mybir.dt.uint8
+FP8X4 = mybir.dt.float8_e4m3fn_x4
+
+P = 128
+PACK = 4
+SPAN = P * PACK
+PASSES = D // SPAN
+GROUPS = F // SPAN
+UNITS = E * GROUPS
+
+
+def tile_expert_up_silu_clip_g2_kernel(tc, x, w_up, ch_scale, ch_limit, out_0, out_1, out_2):
+    nc = tc.nc
+    words_out = out_1.rearrange("g p m t -> g p (m t)").bitcast(I32)
+    scales_out = out_2.bitcast(I32)
+
+    with ExitStack() as ctx:
+        keep = ctx.enter_context(tc.tile_pool(name="keep", bufs=1))
+        work = ctx.enter_context(tc.tile_pool(name="work", bufs=2))
+        psum = ctx.enter_context(tc.psum_pool(name="psum", bufs=2))
+        ctx.enter_context(tc.manual_schedule())
+
+        ident = keep.tile([P, P], F32, name="ident")
+        rows = keep.tile([P, SPAN], BF16, name="rows")
+        consts = keep.tile([P, 2 * UNITS, PACK], F32, name="consts")
+        plane_head = keep.tile([P, GROUPS, (E - 1) * C], U8, name="plane_head", align_bytes=64)
+        plane_last = keep.tile([P, GROUPS, C], U8, name="plane_last", align_bytes=64)
+
+        w_raw = {}
+        x_raw = {}
+        x_bank = {}
+        x_grouped = {}
+        x_mx = {}
+        w_grouped = {}
+        w_mx = {}
+        acc = {}
+        y = {}
+        y_grouped = {}
+
+        def load_w_group(g, k):
+            t = keep.tile([P, PACK, SPAN], BF16, name="w_first_%d_%d" % (g, k))
+            src = w_up[0, k * SPAN:(k + 1) * SPAN, g * SPAN:(g + 1) * SPAN]
+            nc.sync.dma_start(out=t[:], in_=src.rearrange("(p j) f -> p j f", j=PACK))
+            w_raw[(g, k)] = t[:]
+
+        def load_w_expert(e, k):
+            t = work.tile([P, PACK, F], BF16, name="w_rest", bufs=4)
+            src = w_up[e, k * SPAN:(k + 1) * SPAN, :]
+            nc.sync.dma_start(out=t[:], in_=src.rearrange("(p j) f -> p j f", j=PACK))
+            for g in range(GROUPS):
+                w_raw[(e * GROUPS + g, k)] = t[:, :, g * SPAN:(g + 1) * SPAN]
+
+        def load_x(e, h):
+            t = work.tile([P, 2, D], BF16, name="x_half", bufs=6)
+            src = x[e].rearrange("(m r) d -> m r d", r=PACK)
+            nc.sync.dma_start(out=t[:], in_=src[:, 2 * h:2 * h + 2, :])
+            x_raw[(e, h)] = t
+
+        def transpose_x(e, k, h):
+            bank = psum.tile([P, PACK, P], F32, name="x_bank", bufs=2)
+            words = x_raw[(e, h)][:].bitcast(F32)
+            for r in range(2):
+                for u in range(2):
+                    nc.tensor.transpose(bank[:, 2 * r + u, :], words[:, r, 2 * P * k + u:2 * P * (k + 1):2], ident[:])
+            x_bank[(e, k, h)] = bank
+
+        def copy_x(e, k, h):
+            if h == 0:
+                x_grouped[(e, k)] = work.tile([P, C * PACK], BF16, name="x_grouped", bufs=2, align_bytes=64)
+            dst = x_grouped[(e, k)][:].bitcast(F32).rearrange("p (m h q) -> p m h q", h=2, q=PACK)
+            nc.scalar.copy(out=dst[:, :, h, :], in_=x_bank[(e, k, h)][:].rearrange("p q m -> p m q"))
+
+        def quantize_x(e, k):
+            codes = work.tile([P, C], U32, name="x_codes", bufs=4, align_bytes=64)
+            scales = work.tile([P, C], U8, name="x_scales", bufs=4, align_bytes=64)
+            nc.vector.quantize_mx(out=codes[:].bitcast(FP8X4), scales=scales[:], in_=x_grouped[(e, k)][:])
+            x_mx[(e, k)] = (codes, scales)
+
+        def group_w(s, k, on_vector):
+            t = work.tile([P, SPAN * PACK], BF16, name="w_grouped_%d" % k, bufs=2, align_bytes=64)
+            dst = t[:].rearrange("p (t m j) -> p m t j", t=PACK, j=PACK)
+            src = w_raw[(s, k)].rearrange("p j (m t) -> p m t j", t=PACK)
+            if on_vector:
+                nc.vector.tensor_copy(out=dst, in_=src)
+            else:
+                nc.scalar.copy(out=dst, in_=src)
+            w_grouped[(s, k)] = t
+
+        def quantize_w(s, k):
+            codes = work.tile([P, SPAN], U32, name="w_codes_%d" % k, bufs=2, align_bytes=64)
+            scales = work.tile([P, SPAN], U8, name="w_scales_%d" % k, bufs=2, align_bytes=64)
+            nc.vector.quantize_mx(out=codes[:].bitcast(FP8X4), scales=scales[:], in_=w_grouped[(s, k)][:])
+            w_mx[(s, k)] = (codes, scales)
+
+        def multiply(s):
+            e = s // GROUPS
+            for t in range(PACK):
+                bank = psum.tile([P, C], F32, name="acc", bufs=6)
+                cols = slice(t * P, (t + 1) * P)
+                for k in range(PASSES):
+                    nc.tensor.matmul_mx(
+                        out=bank[:],
+                        lhsT=w_mx[(s, k)][0][:, cols].bitcast(FP8X4),
+                        lhsT_scale=w_mx[(s, k)][1][:, cols],
+                        rhs=x_mx[(e, k)][0][:].bitcast(FP8X4),
+                        rhs_scale=x_mx[(e, k)][1][:],
+                        start=(k == 0),
+                        stop=(k == PASSES - 1),
+                    )
+                acc[(s, t)] = bank
+
+        def silu(s):
+            y[s] = work.tile([P, PACK, C], F32, name="y", bufs=5)
+            for t in range(PACK):
+                nc.scalar.activation(
+                    out=y[s][:, t, :],
+                    in_=acc[(s, t)][:],
+                    func=mybir.ActivationFunctionType.Silu,
+                    scale=consts[:, s, t:t + 1],
+                )
+
+        def clip_and_store(s):
+            e, g = divmod(s, GROUPS)
+            for t in range(PACK):
+                nc.vector.tensor_scalar_min(out=y[s][:, t, :], in0=y[s][:, t, :], scalar1=consts[:, UNITS + s, t:t + 1])
+            dst = out_0[e, g * SPAN:(g + 1) * SPAN, :].rearrange("(p t) c -> p t c", t=PACK)
+            nc.sync.dma_start(out=dst, in_=y[s][:])
+
+        def group_y(s):
+            t = work.tile([P, C * PACK], BF16, name="y_grouped", bufs=2, align_bytes=64)
+            nc.vector.tensor_copy(
+                out=t[:].rearrange("p (c i t) -> p c t i", i=4, t=PACK),
+                in_=y[s][:].rearrange("p t (c i) -> p c t i", i=4),
+            )
+            y_grouped[s] = t
+
+        def quantize_y_and_store(s):
+            e, g = divmod(s, GROUPS)
+            codes = work.tile([P, C], U32, name="y_codes", bufs=3, align_bytes=64)
+            scales = plane_last[:, g, :] if e == E - 1 else plane_head[:, g, e * C:(e + 1) * C]
+            nc.vector.quantize_mx(out=codes[:].bitcast(FP8X4), scales=scales, in_=y_grouped[s][:])
+            nc.sync.dma_start(out=words_out[g, :, e * C:(e + 1) * C], in_=codes[:].bitcast(I32))
+
+        def store_scales(plane, first, count):
+            for q in range(4):
+                dst = scales_out[:, 4 * q:4 * q + 4, first // 4:(first + count) // 4].rearrange("g r m -> r g m")
+                nc.sync.dma_start(out=dst, in_=plane[32 * q:32 * q + 4, :, :].bitcast(I32))
+
+        load_w_group(0, 0)
+        load_x(0, 0)
+        load_w_group(0, 1)
+        load_x(0, 1)
+        for g in range(1, GROUPS):
+            for k in range(PASSES):
+                load_w_group(g, k)
+        nc.vector.memset(rows[:], 0.0)
+        make_identity(nc, ident[:])
+        nc.scalar.dma_start(out=rows[0:UNITS, :], in_=ch_scale.rearrange("e (g f) -> (e g) f", f=SPAN))
+        nc.scalar.dma_start(out=rows[UNITS:2 * UNITS, :], in_=ch_limit.rearrange("e (g f) -> (e g) f", f=SPAN))
+        load_x(1, 0)
+        load_x(1, 1)
+        load_w_expert(1, 0)
+        load_w_expert(1, 1)
+
+        group_w(0, 0, True)
+        for k in range(PASSES):
+            transpose_x(0, k, 0)
+        for k in range(PASSES):
+            copy_x(0, k, 0)
+        const_bank = psum.tile([P, 2, P], F32, name="acc", bufs=6)
+        for u in range(2):
+            nc.tensor.transpose(const_bank[:, u, :], rows[:].bitcast(F32)[:, u:2 * P:2], ident[:])
+        group_w(0, 1, True)
+        for k in range(PASSES):
+            transpose_x(0, k, 1)
+        for k in range(PASSES):
+            copy_x(0, k, 1)
+        nc.vector.tensor_copy(
+            out=consts[:].rearrange("p r (u h) -> p u r h", h=2),
+            in_=const_bank[:].bitcast(BF16).rearrange("p u (r h) -> p u r h", h=2)[:, :, 0:2 * UNITS, :],
+        )
+        for k in range(PASSES):
+            quantize_w(0, k)
+        for k in range(PASSES):
+            quantize_x(0, k)
+        multiply(0)
+        group_w(1, 0, True)
+        group_w(1, 1, False)
+
+        for i in range(UNITS + 2):
+            e, g = divmod(i, GROUPS)
+            if g == 0 and e + 2 < E:
+                load_x(e + 2, 0)
+                load_x(e + 2, 1)
+            if i == 0 or i == GROUPS + 1:
+                load_w_expert(e + 2, 0)
+            if i == 1 or i == GROUPS + 1:
+                load_w_expert(e + 2, 1)
+            x_next = e + 1 < E
+            if x_next and g < PASSES:
+                transpose_x(e + 1, g, 0)
+                transpose_x(e + 1, g, 1)
+            if 0 <= i - 2:
+                quantize_y_and_store(i - 2)
+                if i - 2 == UNITS - GROUPS - 1:
+                    store_scales(plane_head, 0, (E - 1) * C)
+            if 0 <= i - 1 < UNITS:
+                clip_and_store(i - 1)
+            if i < UNITS:
+                silu(i)
+            if x_next and g >= 1:
+                quantize_x(e + 1, g - 1)
+            if i + 1 < UNITS:
+                for k in range(PASSES):
+                    quantize_w(i + 1, k)
+                multiply(i + 1)
+            if x_next and g < PASSES:
+                copy_x(e + 1, g, 0)
+                copy_x(e + 1, g, 1)
+            if 0 <= i - 1 < UNITS:
+                group_y(i - 1)
+            if i + 2 < UNITS:
+                group_w(i + 2, 0, True)
+                group_w(i + 2, 1, False)
+        store_scales(plane_last, (E - 1) * C, C)

@@ -12,6 +12,7 @@ U32 = mybir.dt.uint32
 I32 = mybir.dt.int32
 U8 = mybir.dt.uint8
 FP8X4 = mybir.dt.float8_e4m3fn_x4
+SILU = mybir.ActivationFunctionType.Silu
 
 P = 128
 PACK = 4
@@ -19,6 +20,11 @@ SPAN = P * PACK
 PASSES = D // SPAN
 GROUPS = F // SPAN
 UNITS = E * GROUPS
+PAIR = 2
+FREE_BANKS = 2
+
+HEAD_SLOTS = 2
+TAIL_RUNS = {UNITS - 3: 128, UNITS - 2: 64, UNITS - 1: 44}
 
 
 def tile_expert_up_silu_clip_g2_kernel(tc, x, w_up, ch_scale, ch_limit, out_0, out_1, out_2):
@@ -35,42 +41,34 @@ def tile_expert_up_silu_clip_g2_kernel(tc, x, w_up, ch_scale, ch_limit, out_0, o
         ident = keep.tile([P, P], F32, name="ident")
         rows = keep.tile([P, SPAN], BF16, name="rows")
         consts = keep.tile([P, 2 * UNITS, PACK], F32, name="consts")
-        plane_head = keep.tile([P, GROUPS, (E - 1) * C], U8, name="plane_head", align_bytes=64)
-        plane_last = keep.tile([P, GROUPS, C], U8, name="plane_last", align_bytes=64)
+        warm = keep.tile([P, 1], F32, name="warm")
+        y_scales = [keep.tile([P, GROUPS, PAIR * C], U8, name="y_scales_%d" % n, align_bytes=64) for n in range(E // PAIR)]
+        pair_codes = [keep.tile([P, PAIR * C], U32, name="pair_codes_%d" % g, align_bytes=64) for g in range(GROUPS)]
 
-        w_raw = {}
-        x_raw = {}
-        x_bank = {}
-        x_grouped = {}
-        x_mx = {}
-        w_grouped = {}
-        w_mx = {}
-        acc = {}
-        y = {}
-        y_grouped = {}
+        w_raw, w_laid, w_mx = {}, {}, {}
+        x_raw, x_bank, x_laid, x_mx = {}, {}, {}, {}
+        acc, y, y_laid = {}, {}, {}
 
-        def load_w_group(g, k):
-            t = keep.tile([P, PACK, SPAN], BF16, name="w_first_%d_%d" % (g, k))
-            src = w_up[0, k * SPAN:(k + 1) * SPAN, g * SPAN:(g + 1) * SPAN]
-            nc.sync.dma_start(out=t[:], in_=src.rearrange("(p j) f -> p j f", j=PACK))
-            w_raw[(g, k)] = t[:]
+        def load_w(e, k, first, last):
+            width = last - first
+            depth = {1: 4, 2: 2, GROUPS: 4}[width]
+            raw = work.tile([P, PACK, width * SPAN], BF16, name="w_raw_%d" % width, bufs=depth)
+            src = w_up[e, k * SPAN:(k + 1) * SPAN, first * SPAN:last * SPAN]
+            nc.sync.dma_start(out=raw[:], in_=src.rearrange("(p j) f -> p j f", j=PACK))
+            for g in range(first, last):
+                w_raw[(e * GROUPS + g, k)] = raw[:, :, (g - first) * SPAN:(g - first + 1) * SPAN]
 
-        def load_w_expert(e, k):
-            t = work.tile([P, PACK, F], BF16, name="w_rest", bufs=4)
-            src = w_up[e, k * SPAN:(k + 1) * SPAN, :]
-            nc.sync.dma_start(out=t[:], in_=src.rearrange("(p j) f -> p j f", j=PACK))
-            for g in range(GROUPS):
-                w_raw[(e * GROUPS + g, k)] = t[:, :, g * SPAN:(g + 1) * SPAN]
-
-        def load_x(e, h):
-            t = work.tile([P, 2, D], BF16, name="x_half", bufs=6)
+        def load_x(e, first, last):
+            width = last - first
+            raw = work.tile([P, 2 * width, D], BF16, name="x_raw_%d" % width, bufs=2)
             src = x[e].rearrange("(m r) d -> m r d", r=PACK)
-            nc.sync.dma_start(out=t[:], in_=src[:, 2 * h:2 * h + 2, :])
-            x_raw[(e, h)] = t
+            nc.sync.dma_start(out=raw[:], in_=src[:, 2 * first:2 * last, :])
+            for h in range(first, last):
+                x_raw[(e, h)] = raw[:, 2 * (h - first):2 * (h - first) + 2, :]
 
         def transpose_x(e, k, h):
             bank = psum.tile([P, PACK, P], F32, name="x_bank", bufs=2)
-            words = x_raw[(e, h)][:].bitcast(F32)
+            words = x_raw[(e, h)].bitcast(F32)
             for r in range(2):
                 for u in range(2):
                     nc.tensor.transpose(bank[:, 2 * r + u, :], words[:, r, 2 * P * k + u:2 * P * (k + 1):2], ident[:])
@@ -78,36 +76,41 @@ def tile_expert_up_silu_clip_g2_kernel(tc, x, w_up, ch_scale, ch_limit, out_0, o
 
         def copy_x(e, k, h):
             if h == 0:
-                x_grouped[(e, k)] = work.tile([P, C * PACK], BF16, name="x_grouped", bufs=2, align_bytes=64)
-            dst = x_grouped[(e, k)][:].bitcast(F32).rearrange("p (m h q) -> p m h q", h=2, q=PACK)
+                x_laid[(e, k)] = work.tile([P, C * PACK], BF16, name="x_laid", bufs=2, align_bytes=64)
+            dst = x_laid[(e, k)][:].bitcast(F32).rearrange("p (m h q) -> p m h q", h=2, q=PACK)
             nc.scalar.copy(out=dst[:, :, h, :], in_=x_bank[(e, k, h)][:].rearrange("p q m -> p m q"))
 
         def quantize_x(e, k):
-            codes = work.tile([P, C], U32, name="x_codes", bufs=4, align_bytes=64)
-            scales = work.tile([P, C], U8, name="x_scales", bufs=4, align_bytes=64)
-            nc.vector.quantize_mx(out=codes[:].bitcast(FP8X4), scales=scales[:], in_=x_grouped[(e, k)][:])
+            codes = work.tile([P, C], U32, name="x_codes", bufs=2 * PASSES, align_bytes=64)
+            scales = work.tile([P, C], U8, name="x_scales", bufs=2 * PASSES, align_bytes=64)
+            nc.vector.quantize_mx(out=codes[:].bitcast(FP8X4), scales=scales[:], in_=x_laid[(e, k)][:])
             x_mx[(e, k)] = (codes, scales)
 
-        def group_w(s, k, on_vector):
-            t = work.tile([P, SPAN * PACK], BF16, name="w_grouped_%d" % k, bufs=2, align_bytes=64)
-            dst = t[:].rearrange("p (t m j) -> p m t j", t=PACK, j=PACK)
-            src = w_raw[(s, k)].rearrange("p j (m t) -> p m t j", t=PACK)
-            if on_vector:
-                nc.vector.tensor_copy(out=dst, in_=src)
-            else:
-                nc.scalar.copy(out=dst, in_=src)
-            w_grouped[(s, k)] = t
+        def lay_w(copy, s, k, first, last):
+            if (s, k) not in w_laid:
+                w_laid[(s, k)] = work.tile([P, SPAN * PACK], BF16, name="w_laid_%d" % k, bufs=2, align_bytes=64)
+            dst = w_laid[(s, k)][:].rearrange("p (t n i j) -> p n t j i", t=PACK, i=2, j=PACK)
+            src = w_raw[(s, k)].rearrange("p j (n i t) -> p n t j i", t=PACK, i=2)
+            copy(out=dst[:, :, first:last], in_=src[:, :, first:last])
+
+        def scalar_slots(s):
+            return HEAD_SLOTS if s < GROUPS else PACK
+
+        def lay_w_vector(s):
+            lay_w(nc.vector.tensor_copy, s, 0, 0, PACK)
+            if scalar_slots(s) < PACK:
+                lay_w(nc.vector.tensor_copy, s, 1, scalar_slots(s), PACK)
 
         def quantize_w(s, k):
             codes = work.tile([P, SPAN], U32, name="w_codes_%d" % k, bufs=2, align_bytes=64)
             scales = work.tile([P, SPAN], U8, name="w_scales_%d" % k, bufs=2, align_bytes=64)
-            nc.vector.quantize_mx(out=codes[:].bitcast(FP8X4), scales=scales[:], in_=w_grouped[(s, k)][:])
+            nc.vector.quantize_mx(out=codes[:].bitcast(FP8X4), scales=scales[:], in_=w_laid[(s, k)][:])
             w_mx[(s, k)] = (codes, scales)
 
-        def multiply(s):
+        def multiply(s, first, last):
             e = s // GROUPS
-            for t in range(PACK):
-                bank = psum.tile([P, C], F32, name="acc", bufs=6)
+            for t in range(first, last):
+                bank = psum.tile([P, C], F32, name="acc", bufs=PACK + FREE_BANKS)
                 cols = slice(t * P, (t + 1) * P)
                 for k in range(PASSES):
                     nc.tensor.matmul_mx(
@@ -124,114 +127,128 @@ def tile_expert_up_silu_clip_g2_kernel(tc, x, w_up, ch_scale, ch_limit, out_0, o
         def silu(s):
             y[s] = work.tile([P, PACK, C], F32, name="y", bufs=5)
             for t in range(PACK):
-                nc.scalar.activation(
-                    out=y[s][:, t, :],
-                    in_=acc[(s, t)][:],
-                    func=mybir.ActivationFunctionType.Silu,
-                    scale=consts[:, s, t:t + 1],
-                )
+                nc.scalar.activation(out=y[s][:, t, :], in_=acc[(s, t)][:], func=SILU, scale=consts[:, s, t:t + 1])
 
         def clip_and_store(s):
             e, g = divmod(s, GROUPS)
+            dst = out_0[e, g * SPAN:(g + 1) * SPAN, :].rearrange("(p t) c -> p t c", t=PACK)
+            run = PACK // 2 if s == UNITS - 1 else PACK
             for t in range(PACK):
                 nc.vector.tensor_scalar_min(out=y[s][:, t, :], in0=y[s][:, t, :], scalar1=consts[:, UNITS + s, t:t + 1])
-            dst = out_0[e, g * SPAN:(g + 1) * SPAN, :].rearrange("(p t) c -> p t c", t=PACK)
-            nc.sync.dma_start(out=dst, in_=y[s][:])
+                if (t + 1) % run == 0:
+                    nc.sync.dma_start(out=dst[:, t + 1 - run:t + 1, :], in_=y[s][:, t + 1 - run:t + 1, :])
 
-        def group_y(s):
-            t = work.tile([P, C * PACK], BF16, name="y_grouped", bufs=2, align_bytes=64)
-            nc.vector.tensor_copy(
-                out=t[:].rearrange("p (c i t) -> p c t i", i=4, t=PACK),
-                in_=y[s][:].rearrange("p t (c i) -> p c t i", i=4),
-            )
-            y_grouped[s] = t
+        def lay_y(copy, s, first, last):
+            if s not in y_laid:
+                y_laid[s] = work.tile([P, C * PACK], BF16, name="y_laid", bufs=2, align_bytes=64)
+            dst = y_laid[s][:].rearrange("p (n i t) -> p n t i", i=4, t=PACK)
+            src = y[s][:].rearrange("p t (n i) -> p n t i", i=4)
+            copy(out=dst[:, first:last], in_=src[:, first:last])
 
         def quantize_y_and_store(s):
             e, g = divmod(s, GROUPS)
-            codes = work.tile([P, C], U32, name="y_codes", bufs=3, align_bytes=64)
-            scales = plane_last[:, g, :] if e == E - 1 else plane_head[:, g, e * C:(e + 1) * C]
-            nc.vector.quantize_mx(out=codes[:].bitcast(FP8X4), scales=scales, in_=y_grouped[s][:])
-            nc.sync.dma_start(out=words_out[g, :, e * C:(e + 1) * C], in_=codes[:].bitcast(I32))
+            cols = slice((e % PAIR) * C, (e % PAIR + 1) * C)
+            if e < PAIR:
+                codes = pair_codes[g][:, cols]
+            else:
+                single = work.tile([P, C], U32, name="y_codes", bufs=3, align_bytes=64)
+                codes = single[:]
+            nc.vector.quantize_mx(out=codes.bitcast(FP8X4), scales=y_scales[e // PAIR][:, g, cols], in_=y_laid[s][:])
+            if e == PAIR - 1:
+                nc.sync.dma_start(out=words_out[g, :, 0:PAIR * C], in_=pair_codes[g][:].bitcast(I32))
+            if e >= PAIR:
+                nc.sync.dma_start(out=words_out[g, :, e * C:(e + 1) * C], in_=codes.bitcast(I32))
 
-        def store_scales(plane, first, count):
+        def store_scales(queue, n):
+            cols = slice(n * PAIR * C // 4, (n + 1) * PAIR * C // 4)
             for q in range(4):
-                dst = scales_out[:, 4 * q:4 * q + 4, first // 4:(first + count) // 4].rearrange("g r m -> r g m")
-                nc.sync.dma_start(out=dst, in_=plane[32 * q:32 * q + 4, :, :].bitcast(I32))
+                dst = scales_out[:, 4 * q:4 * q + 4, cols].rearrange("g r m -> r g m")
+                queue.dma_start(out=dst, in_=y_scales[n][32 * q:32 * q + 4, :, :].bitcast(I32))
 
-        load_w_group(0, 0)
-        load_x(0, 0)
-        load_w_group(0, 1)
-        load_x(0, 1)
-        for g in range(1, GROUPS):
-            for k in range(PASSES):
-                load_w_group(g, k)
         nc.vector.memset(rows[:], 0.0)
+        nc.scalar.activation(out=warm[:], in_=rows[:, 0:1], func=SILU)
         make_identity(nc, ident[:])
-        nc.scalar.dma_start(out=rows[0:UNITS, :], in_=ch_scale.rearrange("e (g f) -> (e g) f", f=SPAN))
-        nc.scalar.dma_start(out=rows[UNITS:2 * UNITS, :], in_=ch_limit.rearrange("e (g f) -> (e g) f", f=SPAN))
-        load_x(1, 0)
-        load_x(1, 1)
-        load_w_expert(1, 0)
-        load_w_expert(1, 1)
 
-        group_w(0, 0, True)
         for k in range(PASSES):
-            transpose_x(0, k, 0)
-        for k in range(PASSES):
-            copy_x(0, k, 0)
-        const_bank = psum.tile([P, 2, P], F32, name="acc", bufs=6)
+            load_w(0, k, 0, 1)
+            load_x(0, k, k + 1)
+        load_w(0, 0, 1, 2)
+        nc.sync.dma_start(out=rows[0:UNITS, :], in_=ch_scale.rearrange("e (g f) -> (e g) f", f=SPAN))
+        nc.sync.dma_start(out=rows[UNITS:2 * UNITS, :], in_=ch_limit.rearrange("e (g f) -> (e g) f", f=SPAN))
+        load_w(0, 1, 1, GROUPS)
+        load_w(0, 0, 2, GROUPS)
+        for half in range(2):
+            load_x(1, half, half + 1)
+        load_w(1, 1, 0, GROUPS)
+        load_w(1, 0, 0, 1)
+        load_w(1, 0, 1, GROUPS)
+
+        for half in range(2):
+            for k in range(PASSES):
+                transpose_x(0, k, half)
+            for k in range(PASSES):
+                copy_x(0, k, half)
+        const_bank = psum.tile([P, 2, P], F32, name="acc", bufs=PACK + FREE_BANKS)
         for u in range(2):
             nc.tensor.transpose(const_bank[:, u, :], rows[:].bitcast(F32)[:, u:2 * P:2], ident[:])
-        group_w(0, 1, True)
         for k in range(PASSES):
-            transpose_x(0, k, 1)
+            lay_w(nc.vector.tensor_copy, 0, k, 0, PACK)
+            quantize_w(0, k)
+        lay_w(nc.vector.tensor_copy, 1, 0, 0, PACK)
         for k in range(PASSES):
-            copy_x(0, k, 1)
+            quantize_x(0, k)
         nc.vector.tensor_copy(
             out=consts[:].rearrange("p r (u h) -> p u r h", h=2),
             in_=const_bank[:].bitcast(BF16).rearrange("p u (r h) -> p u r h", h=2)[:, :, 0:2 * UNITS, :],
         )
-        for k in range(PASSES):
-            quantize_w(0, k)
-        for k in range(PASSES):
-            quantize_x(0, k)
-        multiply(0)
-        group_w(1, 0, True)
-        group_w(1, 1, False)
+        multiply(0, 0, PACK)
+        lay_w(nc.scalar.copy, 1, 1, 0, HEAD_SLOTS)
+        lay_w(nc.vector.tensor_copy, 1, 1, HEAD_SLOTS, PACK)
 
-        for i in range(UNITS + 2):
+        for i in range(UNITS):
             e, g = divmod(i, GROUPS)
-            if g == 0 and e + 2 < E:
-                load_x(e + 2, 0)
-                load_x(e + 2, 1)
-            if i == 0 or i == GROUPS + 1:
-                load_w_expert(e + 2, 0)
-            if i == 1 or i == GROUPS + 1:
-                load_w_expert(e + 2, 1)
-            x_next = e + 1 < E
-            if x_next and g < PASSES:
-                transpose_x(e + 1, g, 0)
-                transpose_x(e + 1, g, 1)
-            if 0 <= i - 2:
+            turn_x = e + 1 < E and g < PASSES
+            if e + 2 < E:
+                if g == 0:
+                    load_x(e + 2, 0, 2)
+                if g < PASSES:
+                    load_w(e + 2, PASSES - 1 - g, 0, GROUPS)
+            if turn_x:
+                for half in range(2):
+                    transpose_x(e + 1, g, half)
+            silu(i)
+
+            if i >= 2:
                 quantize_y_and_store(i - 2)
-                if i - 2 == UNITS - GROUPS - 1:
-                    store_scales(plane_head, 0, (E - 1) * C)
-            if 0 <= i - 1 < UNITS:
-                clip_and_store(i - 1)
-            if i < UNITS:
-                silu(i)
-            if x_next and g >= 1:
+                if i - 2 == PAIR * GROUPS - 1:
+                    store_scales(nc.sync, 0)
+            if e + 1 < E and g >= 1:
                 quantize_x(e + 1, g - 1)
             if i + 1 < UNITS:
                 for k in range(PASSES):
                     quantize_w(i + 1, k)
-                multiply(i + 1)
-            if x_next and g < PASSES:
-                copy_x(e + 1, g, 0)
-                copy_x(e + 1, g, 1)
-            if 0 <= i - 1 < UNITS:
-                group_y(i - 1)
+            y_runs = TAIL_RUNS.get(i - 1, 0)
+            if i >= 1 and y_runs < P:
+                lay_y(nc.vector.tensor_copy, i - 1, y_runs, P)
             if i + 2 < UNITS:
-                group_w(i + 2, 0, True)
-                group_w(i + 2, 1, False)
-        store_scales(plane_last, (E - 1) * C, C)
+                lay_w_vector(i + 2)
+            clip_and_store(i)
+
+            if i + 1 < UNITS:
+                multiply(i + 1, 0, FREE_BANKS)
+            if turn_x:
+                for half in range(2):
+                    copy_x(e + 1, g, half)
+            if i + 2 < UNITS:
+                lay_w(nc.scalar.copy, i + 2, 1, 0, scalar_slots(i + 2))
+            if y_runs > 0:
+                lay_y(nc.scalar.copy, i - 1, 0, y_runs)
+            if i + 1 < UNITS:
+                multiply(i + 1, FREE_BANKS, PACK)
+
+        last_group = UNITS - 1
+        lay_y(nc.vector.tensor_copy, last_group, TAIL_RUNS[last_group], P)
+        quantize_y_and_store(last_group - 1)
+        lay_y(nc.scalar.copy, last_group, 0, TAIL_RUNS[last_group])
+        quantize_y_and_store(last_group)
+        store_scales(nc.scalar, 1)

from contextlib import ExitStack

import concourse.mybir as mybir
from concourse.masks import make_identity

E, C, D, F = 4, 512, 1024, 1536
FLOPS = 2 * E * C * D * F

F32 = mybir.dt.float32
BF16 = mybir.dt.bfloat16
U32 = mybir.dt.uint32
I32 = mybir.dt.int32
U8 = mybir.dt.uint8
FP8X4 = mybir.dt.float8_e4m3fn_x4
SILU = mybir.ActivationFunctionType.Silu

P = 128
PACK = 4
SPAN = P * PACK
PASSES = D // SPAN
GROUPS = F // SPAN
UNITS = E * GROUPS
PAIR = 2
FREE_BANKS = 2

HEAD_SLOTS = 2
TAIL_RUNS = {UNITS - 3: 128, UNITS - 2: 64, UNITS - 1: 44}


def tile_expert_up_silu_clip_g2_kernel(tc, x, w_up, ch_scale, ch_limit, out_0, out_1, out_2):
    nc = tc.nc
    words_out = out_1.rearrange("g p m t -> g p (m t)").bitcast(I32)
    scales_out = out_2.bitcast(I32)

    with ExitStack() as ctx:
        keep = ctx.enter_context(tc.tile_pool(name="keep", bufs=1))
        work = ctx.enter_context(tc.tile_pool(name="work", bufs=2))
        psum = ctx.enter_context(tc.psum_pool(name="psum", bufs=2))
        ctx.enter_context(tc.manual_schedule())

        ident = keep.tile([P, P], F32, name="ident")
        rows = keep.tile([P, SPAN], BF16, name="rows")
        consts = keep.tile([P, 2 * UNITS, PACK], F32, name="consts")
        warm = keep.tile([P, 1], F32, name="warm")
        y_scales = [keep.tile([P, GROUPS, PAIR * C], U8, name="y_scales_%d" % n, align_bytes=64) for n in range(E // PAIR)]
        pair_codes = [keep.tile([P, PAIR * C], U32, name="pair_codes_%d" % g, align_bytes=64) for g in range(GROUPS)]

        w_raw, w_laid, w_mx = {}, {}, {}
        x_raw, x_bank, x_laid, x_mx = {}, {}, {}, {}
        acc, y, y_laid = {}, {}, {}

        def load_w(e, k, first, last):
            width = last - first
            depth = {1: 4, 2: 2, GROUPS: 4}[width]
            raw = work.tile([P, PACK, width * SPAN], BF16, name="w_raw_%d" % width, bufs=depth)
            src = w_up[e, k * SPAN:(k + 1) * SPAN, first * SPAN:last * SPAN]
            nc.sync.dma_start(out=raw[:], in_=src.rearrange("(p j) f -> p j f", j=PACK))
            for g in range(first, last):
                w_raw[(e * GROUPS + g, k)] = raw[:, :, (g - first) * SPAN:(g - first + 1) * SPAN]

        def load_x(e, first, last):
            width = last - first
            raw = work.tile([P, 2 * width, D], BF16, name="x_raw_%d" % width, bufs=2)
            src = x[e].rearrange("(m r) d -> m r d", r=PACK)
            nc.sync.dma_start(out=raw[:], in_=src[:, 2 * first:2 * last, :])
            for h in range(first, last):
                x_raw[(e, h)] = raw[:, 2 * (h - first):2 * (h - first) + 2, :]

        def transpose_x(e, k, h):
            bank = psum.tile([P, PACK, P], F32, name="x_bank", bufs=2)
            words = x_raw[(e, h)].bitcast(F32)
            for r in range(2):
                for u in range(2):
                    nc.tensor.transpose(bank[:, 2 * r + u, :], words[:, r, 2 * P * k + u:2 * P * (k + 1):2], ident[:])
            x_bank[(e, k, h)] = bank

        def copy_x(e, k, h):
            if h == 0:
                x_laid[(e, k)] = work.tile([P, C * PACK], BF16, name="x_laid", bufs=2, align_bytes=64)
            dst = x_laid[(e, k)][:].bitcast(F32).rearrange("p (m h q) -> p m h q", h=2, q=PACK)
            nc.scalar.copy(out=dst[:, :, h, :], in_=x_bank[(e, k, h)][:].rearrange("p q m -> p m q"))

        def quantize_x(e, k):
            codes = work.tile([P, C], U32, name="x_codes", bufs=2 * PASSES, align_bytes=64)
            scales = work.tile([P, C], U8, name="x_scales", bufs=2 * PASSES, align_bytes=64)
            nc.vector.quantize_mx(out=codes[:].bitcast(FP8X4), scales=scales[:], in_=x_laid[(e, k)][:])
            x_mx[(e, k)] = (codes, scales)

        def lay_w(copy, s, k, first, last):
            if (s, k) not in w_laid:
                w_laid[(s, k)] = work.tile([P, SPAN * PACK], BF16, name="w_laid_%d" % k, bufs=2, align_bytes=64)
            dst = w_laid[(s, k)][:].rearrange("p (t n i j) -> p n t j i", t=PACK, i=2, j=PACK)
            src = w_raw[(s, k)].rearrange("p j (n i t) -> p n t j i", t=PACK, i=2)
            copy(out=dst[:, :, first:last], in_=src[:, :, first:last])

        def scalar_slots(s):
            return HEAD_SLOTS if s < GROUPS else PACK

        def lay_w_vector(s):
            lay_w(nc.vector.tensor_copy, s, 0, 0, PACK)
            if scalar_slots(s) < PACK:
                lay_w(nc.vector.tensor_copy, s, 1, scalar_slots(s), PACK)

        def quantize_w(s, k):
            codes = work.tile([P, SPAN], U32, name="w_codes_%d" % k, bufs=2, align_bytes=64)
            scales = work.tile([P, SPAN], U8, name="w_scales_%d" % k, bufs=2, align_bytes=64)
            nc.vector.quantize_mx(out=codes[:].bitcast(FP8X4), scales=scales[:], in_=w_laid[(s, k)][:])
            w_mx[(s, k)] = (codes, scales)

        def multiply(s, first, last):
            e = s // GROUPS
            for t in range(first, last):
                bank = psum.tile([P, C], F32, name="acc", bufs=PACK + FREE_BANKS)
                cols = slice(t * P, (t + 1) * P)
                for k in range(PASSES):
                    nc.tensor.matmul_mx(
                        out=bank[:],
                        lhsT=w_mx[(s, k)][0][:, cols].bitcast(FP8X4),
                        lhsT_scale=w_mx[(s, k)][1][:, cols],
                        rhs=x_mx[(e, k)][0][:].bitcast(FP8X4),
                        rhs_scale=x_mx[(e, k)][1][:],
                        start=(k == 0),
                        stop=(k == PASSES - 1),
                    )
                acc[(s, t)] = bank

        def silu(s):
            y[s] = work.tile([P, PACK, C], F32, name="y", bufs=5)
            for t in range(PACK):
                nc.scalar.activation(out=y[s][:, t, :], in_=acc[(s, t)][:], func=SILU, scale=consts[:, s, t:t + 1])

        def clip_and_store(s):
            e, g = divmod(s, GROUPS)
            dst = out_0[e, g * SPAN:(g + 1) * SPAN, :].rearrange("(p t) c -> p t c", t=PACK)
            run = PACK // 2 if s == UNITS - 1 else PACK
            for t in range(PACK):
                nc.vector.tensor_scalar_min(out=y[s][:, t, :], in0=y[s][:, t, :], scalar1=consts[:, UNITS + s, t:t + 1])
                if (t + 1) % run == 0:
                    nc.sync.dma_start(out=dst[:, t + 1 - run:t + 1, :], in_=y[s][:, t + 1 - run:t + 1, :])

        def lay_y(copy, s, first, last):
            if s not in y_laid:
                y_laid[s] = work.tile([P, C * PACK], BF16, name="y_laid", bufs=2, align_bytes=64)
            dst = y_laid[s][:].rearrange("p (n i t) -> p n t i", i=4, t=PACK)
            src = y[s][:].rearrange("p t (n i) -> p n t i", i=4)
            copy(out=dst[:, first:last], in_=src[:, first:last])

        def quantize_y_and_store(s):
            e, g = divmod(s, GROUPS)
            cols = slice((e % PAIR) * C, (e % PAIR + 1) * C)
            if e < PAIR:
                codes = pair_codes[g][:, cols]
            else:
                single = work.tile([P, C], U32, name="y_codes", bufs=3, align_bytes=64)
                codes = single[:]
            nc.vector.quantize_mx(out=codes.bitcast(FP8X4), scales=y_scales[e // PAIR][:, g, cols], in_=y_laid[s][:])
            if e == PAIR - 1:
                nc.sync.dma_start(out=words_out[g, :, 0:PAIR * C], in_=pair_codes[g][:].bitcast(I32))
            if e >= PAIR:
                nc.sync.dma_start(out=words_out[g, :, e * C:(e + 1) * C], in_=codes.bitcast(I32))

        def store_scales(queue, n):
            cols = slice(n * PAIR * C // 4, (n + 1) * PAIR * C // 4)
            for q in range(4):
                dst = scales_out[:, 4 * q:4 * q + 4, cols].rearrange("g r m -> r g m")
                queue.dma_start(out=dst, in_=y_scales[n][32 * q:32 * q + 4, :, :].bitcast(I32))

        nc.vector.memset(rows[:], 0.0)
        nc.scalar.activation(out=warm[:], in_=rows[:, 0:1], func=SILU)
        make_identity(nc, ident[:])

        for k in range(PASSES):
            load_w(0, k, 0, 1)
            load_x(0, k, k + 1)
        load_w(0, 0, 1, 2)
        nc.sync.dma_start(out=rows[0:UNITS, :], in_=ch_scale.rearrange("e (g f) -> (e g) f", f=SPAN))
        nc.sync.dma_start(out=rows[UNITS:2 * UNITS, :], in_=ch_limit.rearrange("e (g f) -> (e g) f", f=SPAN))
        load_w(0, 1, 1, GROUPS)
        load_w(0, 0, 2, GROUPS)
        for half in range(2):
            load_x(1, half, half + 1)
        load_w(1, 1, 0, GROUPS)
        load_w(1, 0, 0, 1)
        load_w(1, 0, 1, GROUPS)

        for half in range(2):
            for k in range(PASSES):
                transpose_x(0, k, half)
            for k in range(PASSES):
                copy_x(0, k, half)
        const_bank = psum.tile([P, 2, P], F32, name="acc", bufs=PACK + FREE_BANKS)
        for u in range(2):
            nc.tensor.transpose(const_bank[:, u, :], rows[:].bitcast(F32)[:, u:2 * P:2], ident[:])
        for k in range(PASSES):
            lay_w(nc.vector.tensor_copy, 0, k, 0, PACK)
            quantize_w(0, k)
        lay_w(nc.vector.tensor_copy, 1, 0, 0, PACK)
        for k in range(PASSES):
            quantize_x(0, k)
        nc.vector.tensor_copy(
            out=consts[:].rearrange("p r (u h) -> p u r h", h=2),
            in_=const_bank[:].bitcast(BF16).rearrange("p u (r h) -> p u r h", h=2)[:, :, 0:2 * UNITS, :],
        )
        multiply(0, 0, PACK)
        lay_w(nc.scalar.copy, 1, 1, 0, HEAD_SLOTS)
        lay_w(nc.vector.tensor_copy, 1, 1, HEAD_SLOTS, PACK)

        for i in range(UNITS):
            e, g = divmod(i, GROUPS)
            turn_x = e + 1 < E and g < PASSES
            if e + 2 < E:
                if g == 0:
                    load_x(e + 2, 0, 2)
                if g < PASSES:
                    load_w(e + 2, PASSES - 1 - g, 0, GROUPS)
            if turn_x:
                for half in range(2):
                    transpose_x(e + 1, g, half)
            silu(i)

            if i >= 2:
                quantize_y_and_store(i - 2)
                if i - 2 == PAIR * GROUPS - 1:
                    store_scales(nc.sync, 0)
            if e + 1 < E and g >= 1:
                quantize_x(e + 1, g - 1)
            if i + 1 < UNITS:
                for k in range(PASSES):
                    quantize_w(i + 1, k)
            y_runs = TAIL_RUNS.get(i - 1, 0)
            if i >= 1 and y_runs < P:
                lay_y(nc.vector.tensor_copy, i - 1, y_runs, P)
            if i + 2 < UNITS:
                lay_w_vector(i + 2)
            clip_and_store(i)

            if i + 1 < UNITS:
                multiply(i + 1, 0, FREE_BANKS)
            if turn_x:
                for half in range(2):
                    copy_x(e + 1, g, half)
            if i + 2 < UNITS:
                lay_w(nc.scalar.copy, i + 2, 1, 0, scalar_slots(i + 2))
            if y_runs > 0:
                lay_y(nc.scalar.copy, i - 1, 0, y_runs)
            if i + 1 < UNITS:
                multiply(i + 1, FREE_BANKS, PACK)

        last_group = UNITS - 1
        lay_y(nc.vector.tensor_copy, last_group, TAIL_RUNS[last_group], P)
        quantize_y_and_store(last_group - 1)
        lay_y(nc.scalar.copy, last_group, 0, TAIL_RUNS[last_group])
        quantize_y_and_store(last_group)
        store_scales(nc.scalar, 1)
